import numpy as np
import ml_dtypes

BF16 = ml_dtypes.bfloat16


def bf(x):
    return np.asarray(x, np.float32).astype(BF16)


def f32(x):
    return np.asarray(x, np.float32)


def f64(x):
    return np.asarray(x).astype(np.float64)


def striped(idx):
    return np.concatenate([l.reshape(-1, 16).T for l in idx])


def rows(idx, k):
    return np.tile(np.repeat(idx, 16, axis=0), (k // (16 * 8), 1))


def look(tab, idx):
    return np.take_along_axis(f64(tab), rows(idx, len(tab)), axis=1)


K, S, V, N = 256, 2048, 2048, 2048


def silu(v):
    return v / (1.0 + np.exp(-v))


def setup_inputs():
    return {"tab": f32(np.random.standard_normal((2, K, S))), "offs": striped(np.stack([np.random.permutation(S)[:N] for _ in range(8)]))}


def reference(tab, offs):
    idx = np.stack([g.T.reshape(-1) for g in np.split(offs, 8)])
    x = silu(look(tab[0], idx)) * look(tab[1], idx)
    return x

@@ -1,0 +1,42 @@
+import concourse.mybir as mybir
+
+F32 = mybir.dt.float32
+U16 = mybir.dt.uint16
+
+P = 128
+LANES = 16
+PIECE = 512
+
+
+def tile_lookup_glu_silu_out_kernel(tc, tab, offs, out):
+    nc = tc.nc
+    rows, places = tab.shape[1], tab.shape[2]
+    entries = out.shape[1]
+    blocks = rows // P
+    pieces = entries // PIECE
+    cols = PIECE // LANES
+
+    with (
+        tc.tile_pool(name="held", bufs=1) as held,
+        tc.tile_pool(name="work", bufs=blocks * pieces) as work,
+    ):
+        offsets = held.tile([P, entries // LANES], U16, name="offsets")
+        nc.sync.dma_start(offsets[:], offs)
+
+        gates, values = [], []
+        for b in range(blocks):
+            gate = held.tile([P, places], F32, name=f"gate{b}")
+            value = held.tile([P, places], F32, name=f"value{b}")
+            nc.sync.dma_start(gate[:], tab[0, b * P : (b + 1) * P, :])
+            nc.sync.dma_start(value[:], tab[1, b * P : (b + 1) * P, :])
+            gates.append(gate)
+            values.append(value)
+
+        for b in range(blocks):
+            for i in range(pieces):
+                picks = offsets[:, i * cols : (i + 1) * cols]
+                silu = work.tile([P, PIECE], F32, name="silu")
+                gated = work.tile([P, PIECE], F32, name="gated")
+                nc.scalar.activation(silu[:], gates[b][:].indirect(picks), mybir.ActivationFunctionType.Silu)
+                nc.vector.tensor_tensor(gated[:], values[b][:].indirect(picks), silu[:], mybir.AluOpType.mult)
+                nc.sync.dma_start(out[b * P : (b + 1) * P, i * PIECE : (i + 1) * PIECE], gated[:])

@@ -23,6 +23,11 @@ def tile_lookup_glu_silu_out_kernel(tc, tab, offs, out):
         offsets = held.tile([P, entries // LANES], U16, name="offsets")
         nc.sync.dma_start(offsets[:], offs)
 
+        zero = held.tile([P, 1], F32, name="zero")
+        warm = held.tile([P, 1], F32, name="warm")
+        nc.vector.memset(zero[:], 0.0)
+        nc.scalar.activation(warm[:], zero[:], mybir.ActivationFunctionType.Silu)
+
         gates, values = [], []
         for b in range(blocks):
             gate = held.tile([P, places], F32, name=f"gate{b}")

@@ -6,6 +6,7 @@ U16 = mybir.dt.uint16
 P = 128
 LANES = 16
 PIECE = 512
+TAIL = 128
 
 
 def tile_lookup_glu_silu_out_kernel(tc, tab, offs, out):
@@ -14,7 +15,6 @@ def tile_lookup_glu_silu_out_kernel(tc, tab, offs, out):
     entries = out.shape[1]
     blocks = rows // P
     pieces = entries // PIECE
-    cols = PIECE // LANES
 
     with (
         tc.tile_pool(name="held", bufs=1) as held,
@@ -37,11 +37,24 @@ def tile_lookup_glu_silu_out_kernel(tc, tab, offs, out):
             gates.append(gate)
             values.append(value)
 
+        def silu_of(b, first):
+            silu = work.tile([P, PIECE], F32, name="silu")
+            picks = offsets[:, first // LANES : (first + PIECE) // LANES]
+            nc.scalar.activation(silu[:], gates[b][:].indirect(picks), mybir.ActivationFunctionType.Silu)
+            return silu
+
+        def product_out(b, first, factor):
+            count = factor.shape[1]
+            gated = work.tile([P, count], F32, name=f"gated{count}")
+            picks = offsets[:, first // LANES : (first + count) // LANES]
+            nc.vector.tensor_tensor(gated[:], values[b][:].indirect(picks), factor, mybir.AluOpType.mult)
+            nc.sync.dma_start(out[b * P : (b + 1) * P, first : first + count], gated[:])
+
         for b in range(blocks):
-            for i in range(pieces):
-                picks = offsets[:, i * cols : (i + 1) * cols]
-                silu = work.tile([P, PIECE], F32, name="silu")
-                gated = work.tile([P, PIECE], F32, name="gated")
-                nc.scalar.activation(silu[:], gates[b][:].indirect(picks), mybir.ActivationFunctionType.Silu)
-                nc.vector.tensor_tensor(gated[:], values[b][:].indirect(picks), silu[:], mybir.AluOpType.mult)
-                nc.sync.dma_start(out[b * P : (b + 1) * P, i * PIECE : (i + 1) * PIECE], gated[:])
+            for first in range(0, entries, PIECE):
+                silu = silu_of(b, first)
+                if b < blocks - 1 or first + PIECE < entries:
+                    product_out(b, first, silu[:])
+                else:
+                    product_out(b, first, silu[:, : PIECE - TAIL])
+                    product_out(b, first + PIECE - TAIL, silu[:, PIECE - TAIL :])

@@ -21,7 +21,6 @@ def tile_lookup_glu_silu_out_kernel(tc, tab, offs, out):
         tc.tile_pool(name="work", bufs=blocks * pieces) as work,
     ):
         offsets = held.tile([P, entries // LANES], U16, name="offsets")
-        nc.sync.dma_start(offsets[:], offs)
 
         zero = held.tile([P, 1], F32, name="zero")
         warm = held.tile([P, 1], F32, name="warm")
@@ -33,6 +32,8 @@ def tile_lookup_glu_silu_out_kernel(tc, tab, offs, out):
             gate = held.tile([P, places], F32, name=f"gate{b}")
             value = held.tile([P, places], F32, name=f"value{b}")
             nc.sync.dma_start(gate[:], tab[0, b * P : (b + 1) * P, :])
+            if b == 0:
+                nc.sync.dma_start(offsets[:], offs)
             nc.sync.dma_start(value[:], tab[1, b * P : (b + 1) * P, :])
             gates.append(gate)
             values.append(value)

@@ -5,8 +5,13 @@ U16 = mybir.dt.uint16
 
 P = 128
 LANES = 16
-PIECE = 512
-TAIL = 128
+SILU_WIDTHS = ((512, 512, 512, 512), (512, 512, 512, 512))
+PRODUCT_WIDTHS = ((512, 512, 512, 512), (512, 512, 512, 384, 128))
+
+
+def runs(widths):
+    ends = [sum(widths[: i + 1]) for i in range(len(widths))]
+    return list(zip([0] + ends[:-1], ends))
 
 
 def tile_lookup_glu_silu_out_kernel(tc, tab, offs, out):
@@ -14,12 +19,8 @@ def tile_lookup_glu_silu_out_kernel(tc, tab, offs, out):
     rows, places = tab.shape[1], tab.shape[2]
     entries = out.shape[1]
     blocks = rows // P
-    pieces = entries // PIECE
 
-    with (
-        tc.tile_pool(name="held", bufs=1) as held,
-        tc.tile_pool(name="work", bufs=blocks * pieces) as work,
-    ):
+    with tc.tile_pool(name="held", bufs=1) as held:
         offsets = held.tile([P, entries // LANES], U16, name="offsets")
 
         zero = held.tile([P, 1], F32, name="zero")
@@ -38,24 +39,17 @@ def tile_lookup_glu_silu_out_kernel(tc, tab, offs, out):
             gates.append(gate)
             values.append(value)
 
-        def silu_of(b, first):
-            silu = work.tile([P, PIECE], F32, name="silu")
-            picks = offsets[:, first // LANES : (first + PIECE) // LANES]
-            nc.scalar.activation(silu[:], gates[b][:].indirect(picks), mybir.ActivationFunctionType.Silu)
-            return silu
-
-        def product_out(b, first, factor):
-            count = factor.shape[1]
-            gated = work.tile([P, count], F32, name=f"gated{count}")
-            picks = offsets[:, first // LANES : (first + count) // LANES]
-            nc.vector.tensor_tensor(gated[:], values[b][:].indirect(picks), factor, mybir.AluOpType.mult)
-            nc.sync.dma_start(out[b * P : (b + 1) * P, first : first + count], gated[:])
-
         for b in range(blocks):
-            for first in range(0, entries, PIECE):
-                silu = silu_of(b, first)
-                if b < blocks - 1 or first + PIECE < entries:
-                    product_out(b, first, silu[:])
-                else:
-                    product_out(b, first, silu[:, : PIECE - TAIL])
-                    product_out(b, first + PIECE - TAIL, silu[:, PIECE - TAIL :])
+            silu = held.tile([P, entries], F32, name=f"silu{b}")
+            gated = held.tile([P, entries], F32, name=f"gated{b}")
+            for first, end in runs(SILU_WIDTHS[b]):
+                picks = offsets[:, first // LANES : end // LANES]
+                nc.scalar.activation(silu[:, first:end], gates[b][:].indirect(picks), mybir.ActivationFunctionType.Silu)
+            for first, end in runs(PRODUCT_WIDTHS[b]):
+                picks = offsets[:, first // LANES : end // LANES]
+                nc.vector.tensor_tensor(
+                    gated[:, first:end], values[b][:].indirect(picks), silu[:, first:end], mybir.AluOpType.mult
+                )
+                after_last_silu = b == blocks - 1 and first >= entries - SILU_WIDTHS[b][-1]
+                queue = nc.scalar if after_last_silu else nc.sync
+                queue.dma_start(out[b * P : (b + 1) * P, first:end], gated[:, first:end])

@@ -2,6 +2,7 @@ import concourse.mybir as mybir
 
 F32 = mybir.dt.float32
 U16 = mybir.dt.uint16
+U32 = mybir.dt.uint32
 
 P = 128
 LANES = 16
@@ -23,10 +24,8 @@ def tile_lookup_glu_silu_out_kernel(tc, tab, offs, out):
     with tc.tile_pool(name="held", bufs=1) as held:
         offsets = held.tile([P, entries // LANES], U16, name="offsets")
 
-        zero = held.tile([P, 1], F32, name="zero")
-        warm = held.tile([P, 1], F32, name="warm")
-        nc.vector.memset(zero[:], 0.0)
-        nc.scalar.activation(warm[:], zero[:], mybir.ActivationFunctionType.Silu)
+        warm = held.tile([P, 1], U32, name="warm")
+        nc.scalar.activation(warm[:], warm[:], mybir.ActivationFunctionType.Silu, scale=0.0)
 
         gates, values = [], []
         for b in range(blocks):
@@ -45,11 +44,11 @@ def tile_lookup_glu_silu_out_kernel(tc, tab, offs, out):
             for first, end in runs(SILU_WIDTHS[b]):
                 picks = offsets[:, first // LANES : end // LANES]
                 nc.scalar.activation(silu[:, first:end], gates[b][:].indirect(picks), mybir.ActivationFunctionType.Silu)
-            for first, end in runs(PRODUCT_WIDTHS[b]):
+            for i, (first, end) in enumerate(runs(PRODUCT_WIDTHS[b])):
                 picks = offsets[:, first // LANES : end // LANES]
                 nc.vector.tensor_tensor(
                     gated[:, first:end], values[b][:].indirect(picks), silu[:, first:end], mybir.AluOpType.mult
                 )
-                after_last_silu = b == blocks - 1 and first >= entries - SILU_WIDTHS[b][-1]
-                queue = nc.scalar if after_last_silu else nc.sync
+                left = len(PRODUCT_WIDTHS[b]) - 1 - i
+                queue = nc.scalar if b == blocks - 1 and left in (1, 2) else nc.sync
                 queue.dma_start(out[b * P : (b + 1) * P, first:end], gated[:, first:end])

@@ -6,13 +6,9 @@ U32 = mybir.dt.uint32
 
 P = 128
 LANES = 16
-SILU_WIDTHS = ((512, 512, 512, 512), (512, 512, 512, 512))
-PRODUCT_WIDTHS = ((512, 512, 512, 512), (512, 512, 512, 384, 128))
-
-
-def runs(widths):
-    ends = [sum(widths[: i + 1]) for i in range(len(widths))]
-    return list(zip([0] + ends[:-1], ends))
+PIECE = 512
+TAIL = 128
+HANDED = 2
 
 
 def tile_lookup_glu_silu_out_kernel(tc, tab, offs, out):
@@ -27,7 +23,7 @@ def tile_lookup_glu_silu_out_kernel(tc, tab, offs, out):
         warm = held.tile([P, 1], U32, name="warm")
         nc.scalar.activation(warm[:], warm[:], mybir.ActivationFunctionType.Silu, scale=0.0)
 
-        gates, values = [], []
+        gates, values, silus, products = [], [], [], []
         for b in range(blocks):
             gate = held.tile([P, places], F32, name=f"gate{b}")
             value = held.tile([P, places], F32, name=f"value{b}")
@@ -37,18 +33,27 @@ def tile_lookup_glu_silu_out_kernel(tc, tab, offs, out):
             nc.sync.dma_start(value[:], tab[1, b * P : (b + 1) * P, :])
             gates.append(gate)
             values.append(value)
+            silus.append(held.tile([P, entries], F32, name=f"silu{b}"))
+            products.append(held.tile([P, entries], F32, name=f"product{b}"))
 
-        for b in range(blocks):
-            silu = held.tile([P, entries], F32, name=f"silu{b}")
-            gated = held.tile([P, entries], F32, name=f"gated{b}")
-            for first, end in runs(SILU_WIDTHS[b]):
-                picks = offsets[:, first // LANES : end // LANES]
-                nc.scalar.activation(silu[:, first:end], gates[b][:].indirect(picks), mybir.ActivationFunctionType.Silu)
-            for i, (first, end) in enumerate(runs(PRODUCT_WIDTHS[b])):
-                picks = offsets[:, first // LANES : end // LANES]
-                nc.vector.tensor_tensor(
-                    gated[:, first:end], values[b][:].indirect(picks), silu[:, first:end], mybir.AluOpType.mult
-                )
-                left = len(PRODUCT_WIDTHS[b]) - 1 - i
-                queue = nc.scalar if b == blocks - 1 and left in (1, 2) else nc.sync
-                queue.dma_start(out[b * P : (b + 1) * P, first:end], gated[:, first:end])
+        def picks(first, end):
+            return offsets[:, first // LANES : end // LANES]
+
+        pieces = [(b, first, first + PIECE) for b in range(blocks) for first in range(0, entries, PIECE)]
+        for b, first, end in pieces:
+            nc.scalar.activation(
+                silus[b][:, first:end], gates[b][:].indirect(picks(first, end)), mybir.ActivationFunctionType.Silu
+            )
+
+        last_block, first, end = pieces[-1]
+        runs = pieces[:-1] + [(last_block, first, end - TAIL), (last_block, end - TAIL, end)]
+        handed = pieces[-1 - HANDED : -1]
+        for b, first, end in runs:
+            nc.vector.tensor_tensor(
+                products[b][:, first:end],
+                values[b][:].indirect(picks(first, end)),
+                silus[b][:, first:end],
+                mybir.AluOpType.mult,
+            )
+            queue = nc.scalar if (b, first, end) in handed else nc.sync
+            queue.dma_start(out[b * P : (b + 1) * P, first:end], products[b][:, first:end])

@@ -6,16 +6,14 @@ U32 = mybir.dt.uint32
 
 P = 128
 LANES = 16
-PIECE = 512
+LONG = 768
 TAIL = 128
-HANDED = 2
 
 
 def tile_lookup_glu_silu_out_kernel(tc, tab, offs, out):
     nc = tc.nc
-    rows, places = tab.shape[1], tab.shape[2]
+    places = tab.shape[2]
     entries = out.shape[1]
-    blocks = rows // P
 
     with tc.tile_pool(name="held", bufs=1) as held:
         offsets = held.tile([P, entries // LANES], U16, name="offsets")
@@ -24,7 +22,7 @@ def tile_lookup_glu_silu_out_kernel(tc, tab, offs, out):
         nc.scalar.activation(warm[:], warm[:], mybir.ActivationFunctionType.Silu, scale=0.0)
 
         gates, values, silus, products = [], [], [], []
-        for b in range(blocks):
+        for b in range(2):
             gate = held.tile([P, places], F32, name=f"gate{b}")
             value = held.tile([P, places], F32, name=f"value{b}")
             nc.sync.dma_start(gate[:], tab[0, b * P : (b + 1) * P, :])
@@ -39,21 +37,37 @@ def tile_lookup_glu_silu_out_kernel(tc, tab, offs, out):
         def picks(first, end):
             return offsets[:, first // LANES : end // LANES]
 
-        pieces = [(b, first, first + PIECE) for b in range(blocks) for first in range(0, entries, PIECE)]
-        for b, first, end in pieces:
+        def silu(b, first, end):
             nc.scalar.activation(
                 silus[b][:, first:end], gates[b][:].indirect(picks(first, end)), mybir.ActivationFunctionType.Silu
             )
 
-        last_block, first, end = pieces[-1]
-        runs = pieces[:-1] + [(last_block, first, end - TAIL), (last_block, end - TAIL, end)]
-        handed = pieces[-1 - HANDED : -1]
-        for b, first, end in runs:
+        def product(b, first, end):
             nc.vector.tensor_tensor(
                 products[b][:, first:end],
                 values[b][:].indirect(picks(first, end)),
                 silus[b][:, first:end],
                 mybir.AluOpType.mult,
             )
-            queue = nc.scalar if (b, first, end) in handed else nc.sync
+
+        def store(queue, b, first, end):
             queue.dma_start(out[b * P : (b + 1) * P, first:end], products[b][:, first:end])
+
+        for b in range(2):
+            silu(b, 0, LONG)
+            silu(b, LONG, 2 * LONG)
+            silu(b, 2 * LONG, entries)
+
+        product(0, 0, LONG)
+        product(0, LONG, 2 * LONG)
+        store(nc.gpsimd, 0, 0, 2 * LONG)
+        product(0, 2 * LONG, entries)
+        store(nc.gpsimd, 0, 2 * LONG, entries)
+        product(1, 0, LONG)
+        store(nc.gpsimd, 1, 0, LONG)
+        product(1, LONG, 2 * LONG)
+        store(nc.sync, 1, LONG, 2 * LONG)
+        product(1, 2 * LONG, entries - TAIL)
+        store(nc.sync, 1, 2 * LONG, entries - TAIL)
+        product(1, entries - TAIL, entries)
+        store(nc.sync, 1, entries - TAIL, entries)

@@ -50,24 +50,20 @@ def tile_lookup_glu_silu_out_kernel(tc, tab, offs, out):
                 mybir.AluOpType.mult,
             )
 
-        def store(queue, b, first, end):
-            queue.dma_start(out[b * P : (b + 1) * P, first:end], products[b][:, first:end])
+        def store(b, first, end):
+            nc.sync.dma_start(out[b * P : (b + 1) * P, first:end], products[b][:, first:end])
 
         for b in range(2):
             silu(b, 0, LONG)
             silu(b, LONG, 2 * LONG)
             silu(b, 2 * LONG, entries)
 
-        product(0, 0, LONG)
-        product(0, LONG, 2 * LONG)
-        store(nc.gpsimd, 0, 0, 2 * LONG)
-        product(0, 2 * LONG, entries)
-        store(nc.gpsimd, 0, 2 * LONG, entries)
-        product(1, 0, LONG)
-        store(nc.gpsimd, 1, 0, LONG)
-        product(1, LONG, 2 * LONG)
-        store(nc.sync, 1, LONG, 2 * LONG)
-        product(1, 2 * LONG, entries - TAIL)
-        store(nc.sync, 1, 2 * LONG, entries - TAIL)
-        product(1, entries - TAIL, entries)
-        store(nc.sync, 1, entries - TAIL, entries)
+        for b in range(2):
+            for first in (0, LONG):
+                product(b, first, first + LONG)
+                store(b, first, first + LONG // 2)
+                store(b, first + LONG // 2, first + LONG)
+            cuts = [2 * LONG, entries] if b == 0 else [2 * LONG, entries - TAIL, entries]
+            for first, end in zip(cuts, cuts[1:]):
+                product(b, first, end)
+                store(b, first, end)

@@ -53,17 +53,21 @@ def tile_lookup_glu_silu_out_kernel(tc, tab, offs, out):
         def store(b, first, end):
             nc.sync.dma_start(out[b * P : (b + 1) * P, first:end], products[b][:, first:end])
 
-        for b in range(2):
-            silu(b, 0, LONG)
-            silu(b, LONG, 2 * LONG)
-            silu(b, 2 * LONG, entries)
+        silu(0, 0, LONG)
+        silu(0, LONG, 2 * LONG)
+        silu(0, 2 * LONG, entries)
+        silu(1, 0, LONG)
+        silu(1, LONG, entries - LONG)
+        silu(1, entries - LONG, entries)
 
+        widths = [(LONG, LONG, 4 * TAIL), (LONG, 4 * TAIL, 3 * TAIL, 2 * TAIL, TAIL)]
         for b in range(2):
-            for first in (0, LONG):
-                product(b, first, first + LONG)
-                store(b, first, first + LONG // 2)
-                store(b, first + LONG // 2, first + LONG)
-            cuts = [2 * LONG, entries] if b == 0 else [2 * LONG, entries - TAIL, entries]
-            for first, end in zip(cuts, cuts[1:]):
-                product(b, first, end)
-                store(b, first, end)
+            first = 0
+            for width in widths[b]:
+                product(b, first, first + width)
+                if width == LONG:
+                    store(b, first, first + LONG // 2)
+                    store(b, first + LONG // 2, first + LONG)
+                else:
+                    store(b, first, first + width)
+                first += width

@@ -6,8 +6,9 @@ U32 = mybir.dt.uint32
 
 P = 128
 LANES = 16
-LONG = 768
-TAIL = 128
+SILUS = (768, 768, 512)
+PRODUCTS = ((768, 768, 512), (768, 512, 384, 256, 128))
+WIDE = 768
 
 
 def tile_lookup_glu_silu_out_kernel(tc, tab, offs, out):
@@ -17,57 +18,50 @@ def tile_lookup_glu_silu_out_kernel(tc, tab, offs, out):
 
     with tc.tile_pool(name="held", bufs=1) as held:
         offsets = held.tile([P, entries // LANES], U16, name="offsets")
-
         warm = held.tile([P, 1], U32, name="warm")
         nc.scalar.activation(warm[:], warm[:], mybir.ActivationFunctionType.Silu, scale=0.0)
 
-        gates, values, silus, products = [], [], [], []
-        for b in range(2):
-            gate = held.tile([P, places], F32, name=f"gate{b}")
-            value = held.tile([P, places], F32, name=f"value{b}")
-            nc.sync.dma_start(gate[:], tab[0, b * P : (b + 1) * P, :])
-            if b == 0:
-                nc.sync.dma_start(offsets[:], offs)
-            nc.sync.dma_start(value[:], tab[1, b * P : (b + 1) * P, :])
-            gates.append(gate)
-            values.append(value)
-            silus.append(held.tile([P, entries], F32, name=f"silu{b}"))
-            products.append(held.tile([P, entries], F32, name=f"product{b}"))
+        gates = [held.tile([P, places], F32, name=f"gate{b}") for b in range(2)]
+        values = [held.tile([P, places], F32, name=f"value{b}") for b in range(2)]
+        silus = [held.tile([P, entries], F32, name=f"silu{b}") for b in range(2)]
+        products = [held.tile([P, entries], F32, name=f"product{b}") for b in range(2)]
+
+        nc.sync.dma_start(gates[0][:], tab[0, 0:P, :])
+        nc.sync.dma_start(offsets[:], offs)
+        nc.sync.dma_start(values[0][:], tab[1, 0:P, :])
+        nc.sync.dma_start(gates[1][:], tab[0, P : 2 * P, :])
+        nc.sync.dma_start(values[1][:], tab[1, P : 2 * P, :])
 
         def picks(first, end):
             return offsets[:, first // LANES : end // LANES]
 
-        def silu(b, first, end):
-            nc.scalar.activation(
-                silus[b][:, first:end], gates[b][:].indirect(picks(first, end)), mybir.ActivationFunctionType.Silu
-            )
-
-        def product(b, first, end):
-            nc.vector.tensor_tensor(
-                products[b][:, first:end],
-                values[b][:].indirect(picks(first, end)),
-                silus[b][:, first:end],
-                mybir.AluOpType.mult,
-            )
-
-        def store(b, first, end):
-            nc.sync.dma_start(out[b * P : (b + 1) * P, first:end], products[b][:, first:end])
-
-        silu(0, 0, LONG)
-        silu(0, LONG, 2 * LONG)
-        silu(0, 2 * LONG, entries)
-        silu(1, 0, LONG)
-        silu(1, LONG, entries - LONG)
-        silu(1, entries - LONG, entries)
-
-        widths = [(LONG, LONG, 4 * TAIL), (LONG, 4 * TAIL, 3 * TAIL, 2 * TAIL, TAIL)]
         for b in range(2):
             first = 0
-            for width in widths[b]:
-                product(b, first, first + width)
-                if width == LONG:
-                    store(b, first, first + LONG // 2)
-                    store(b, first + LONG // 2, first + LONG)
-                else:
-                    store(b, first, first + width)
+            for width in SILUS:
+                nc.scalar.activation(
+                    silus[b][:, first : first + width],
+                    gates[b][:].indirect(picks(first, first + width)),
+                    mybir.ActivationFunctionType.Silu,
+                )
                 first += width
+
+        stores = []
+        for b in range(2):
+            first = 0
+            for width in PRODUCTS[b]:
+                end = first + width
+                nc.vector.tensor_tensor(
+                    products[b][:, first:end],
+                    values[b][:].indirect(picks(first, end)),
+                    silus[b][:, first:end],
+                    mybir.AluOpType.mult,
+                )
+                if width == WIDE:
+                    stores += [(b, first, first + width // 2), (b, first + width // 2, end)]
+                else:
+                    stores.append((b, first, end))
+                first = end
+
+        for k, (b, first, end) in enumerate(stores):
+            queue = nc.scalar if k >= 4 and (len(stores) - k) % 2 == 0 else nc.sync
+            queue.dma_start(out[b * P : (b + 1) * P, first:end], products[b][:, first:end])

@@ -6,8 +6,8 @@ U32 = mybir.dt.uint32
 
 P = 128
 LANES = 16
-SILUS = (768, 768, 512)
-PRODUCTS = ((768, 768, 512), (768, 512, 384, 256, 128))
+SILUS = ((768, 768, 512), (768, 640, 640))
+PRODUCTS = ((768, 768, 512), (768, 640, 320, 192, 128))
 WIDE = 768
 
 
@@ -37,7 +37,7 @@ def tile_lookup_glu_silu_out_kernel(tc, tab, offs, out):
 
         for b in range(2):
             first = 0
-            for width in SILUS:
+            for width in SILUS[b]:
                 nc.scalar.activation(
                     silus[b][:, first : first + width],
                     gates[b][:].indirect(picks(first, first + width)),
@@ -62,6 +62,5 @@ def tile_lookup_glu_silu_out_kernel(tc, tab, offs, out):
                     stores.append((b, first, end))
                 first = end
 
-        for k, (b, first, end) in enumerate(stores):
-            queue = nc.scalar if k >= 4 and (len(stores) - k) % 2 == 0 else nc.sync
-            queue.dma_start(out[b * P : (b + 1) * P, first:end], products[b][:, first:end])
+        for b, first, end in stores:
+            nc.sync.dma_start(out[b * P : (b + 1) * P, first:end], products[b][:, first:end])

@@ -6,9 +6,9 @@ U32 = mybir.dt.uint32
 
 P = 128
 LANES = 16
-SILUS = ((768, 768, 512), (768, 640, 640))
-PRODUCTS = ((768, 768, 512), (768, 640, 320, 192, 128))
-WIDE = 768
+SILUS = ((704, 704, 640), (704, 640, 704))
+PRODUCTS = ((704, 704, 640), (704, 640, 320, 256, 128))
+WIDE = 704
 
 
 def tile_lookup_glu_silu_out_kernel(tc, tab, offs, out):
@@ -45,6 +45,10 @@ def tile_lookup_glu_silu_out_kernel(tc, tab, offs, out):
                 )
                 first += width
 
+        ready = held.tile([P, 2], F32, name="ready")
+        nc.vector.tensor_copy(ready[:, 0:1], silus[0][:, 0:1])
+        nc.vector.tensor_copy(ready[:, 1:2], values[0][:, 0:1])
+
         stores = []
         for b in range(2):
             first = 0
@@ -56,7 +60,7 @@ def tile_lookup_glu_silu_out_kernel(tc, tab, offs, out):
                     silus[b][:, first:end],
                     mybir.AluOpType.mult,
                 )
-                if width == WIDE:
+                if width >= WIDE:
                     stores += [(b, first, first + width // 2), (b, first + width // 2, end)]
                 else:
                     stores.append((b, first, end))

@@ -45,10 +45,6 @@ def tile_lookup_glu_silu_out_kernel(tc, tab, offs, out):
                 )
                 first += width
 
-        ready = held.tile([P, 2], F32, name="ready")
-        nc.vector.tensor_copy(ready[:, 0:1], silus[0][:, 0:1])
-        nc.vector.tensor_copy(ready[:, 1:2], values[0][:, 0:1])
-
         stores = []
         for b in range(2):
             first = 0

@@ -63,4 +63,5 @@ def tile_lookup_glu_silu_out_kernel(tc, tab, offs, out):
                 first = end
 
         for b, first, end in stores:
-            nc.sync.dma_start(out[b * P : (b + 1) * P, first:end], products[b][:, first:end])
+            queue = nc.scalar if b == 1 and end <= WIDE else nc.sync
+            queue.dma_start(out[b * P : (b + 1) * P, first:end], products[b][:, first:end])

@@ -6,9 +6,18 @@ U32 = mybir.dt.uint32
 
 P = 128
 LANES = 16
-SILUS = ((704, 704, 640), (704, 640, 704))
-PRODUCTS = ((704, 704, 640), (704, 640, 320, 256, 128))
-WIDE = 704
+SILUS = ((768, 768, 512), (768, 512, 768))
+PRODUCTS = ((768, 768, 512), (768, 512, 384, 256, 128))
+STORES = ((512, 512, 512, 512), (512, 256, 512, 256, 128, 256, 128))
+
+
+def spans(widths):
+    first = 0
+    cut = []
+    for width in widths:
+        cut.append((first, first + width))
+        first += width
+    return cut
 
 
 def tile_lookup_glu_silu_out_kernel(tc, tab, offs, out):
@@ -32,36 +41,19 @@ def tile_lookup_glu_silu_out_kernel(tc, tab, offs, out):
         nc.sync.dma_start(gates[1][:], tab[0, P : 2 * P, :])
         nc.sync.dma_start(values[1][:], tab[1, P : 2 * P, :])
 
-        def picks(first, end):
-            return offsets[:, first // LANES : end // LANES]
-
         for b in range(2):
-            first = 0
-            for width in SILUS[b]:
+            for first, end in spans(SILUS[b]):
                 nc.scalar.activation(
-                    silus[b][:, first : first + width],
-                    gates[b][:].indirect(picks(first, first + width)),
+                    silus[b][:, first:end],
+                    gates[b][:].indirect(offsets[:, first // LANES : end // LANES]),
                     mybir.ActivationFunctionType.Silu,
                 )
-                first += width
-
-        stores = []
-        for b in range(2):
-            first = 0
-            for width in PRODUCTS[b]:
-                end = first + width
+            for first, end in spans(PRODUCTS[b]):
                 nc.vector.tensor_tensor(
                     products[b][:, first:end],
-                    values[b][:].indirect(picks(first, end)),
+                    values[b][:].indirect(offsets[:, first // LANES : end // LANES]),
                     silus[b][:, first:end],
                     mybir.AluOpType.mult,
                 )
-                if width >= WIDE:
-                    stores += [(b, first, first + width // 2), (b, first + width // 2, end)]
-                else:
-                    stores.append((b, first, end))
-                first = end
-
-        for b, first, end in stores:
-            queue = nc.scalar if b == 1 and end <= WIDE else nc.sync
-            queue.dma_start(out[b * P : (b + 1) * P, first:end], products[b][:, first:end])
+            for first, end in spans(STORES[b]):
+                nc.sync.dma_start(out[b * P : (b + 1) * P, first:end], products[b][:, first:end])

@@ -5,6 +5,7 @@ U16 = mybir.dt.uint16
 U32 = mybir.dt.uint32
 
 P = 128
+BURST = 256
 LANES = 16
 SILUS = ((768, 768, 512), (768, 512, 768))
 PRODUCTS = ((768, 768, 512), (768, 512, 384, 256, 128))
@@ -26,14 +27,14 @@ def tile_lookup_glu_silu_out_kernel(tc, tab, offs, out):
     entries = out.shape[1]
 
     with tc.tile_pool(name="held", bufs=1) as held:
-        offsets = held.tile([P, entries // LANES], U16, name="offsets")
+        offsets = held.tile([P, entries // LANES], U16, name="offsets", align_bytes=BURST)
         warm = held.tile([P, 1], U32, name="warm")
         nc.scalar.activation(warm[:], warm[:], mybir.ActivationFunctionType.Silu, scale=0.0)
 
-        gates = [held.tile([P, places], F32, name=f"gate{b}") for b in range(2)]
-        values = [held.tile([P, places], F32, name=f"value{b}") for b in range(2)]
+        gates = [held.tile([P, places], F32, name=f"gate{b}", align_bytes=BURST) for b in range(2)]
+        values = [held.tile([P, places], F32, name=f"value{b}", align_bytes=BURST) for b in range(2)]
         silus = [held.tile([P, entries], F32, name=f"silu{b}") for b in range(2)]
-        products = [held.tile([P, entries], F32, name=f"product{b}") for b in range(2)]
+        products = [held.tile([P, entries], F32, name=f"product{b}", align_bytes=BURST) for b in range(2)]
 
         nc.sync.dma_start(gates[0][:], tab[0, 0:P, :])
         nc.sync.dma_start(offsets[:], offs)

@@ -7,9 +7,9 @@ U32 = mybir.dt.uint32
 P = 128
 BURST = 256
 LANES = 16
-SILUS = ((768, 768, 512), (768, 512, 768))
-PRODUCTS = ((768, 768, 512), (768, 512, 384, 256, 128))
-STORES = ((512, 512, 512, 512), (512, 256, 512, 256, 128, 256, 128))
+SILUS = ((704, 704, 640), (704, 640, 704))
+PRODUCTS = ((704, 704, 640), (704, 640, 384, 192, 128))
+STORES = ((384, 320, 384, 320, 640), (384, 320, 640, 384, 192, 128))
 
 
 def spans(widths):

@@ -6,6 +6,7 @@ U32 = mybir.dt.uint32
 
 P = 128
 BURST = 256
+SHIFT = 8
 LANES = 16
 SILUS = ((704, 704, 640), (704, 640, 704))
 PRODUCTS = ((704, 704, 640), (704, 640, 384, 192, 128))
@@ -33,7 +34,7 @@ def tile_lookup_glu_silu_out_kernel(tc, tab, offs, out):
 
         gates = [held.tile([P, places], F32, name=f"gate{b}", align_bytes=BURST) for b in range(2)]
         values = [held.tile([P, places], F32, name=f"value{b}", align_bytes=BURST) for b in range(2)]
-        silus = [held.tile([P, entries], F32, name=f"silu{b}") for b in range(2)]
+        silus = [held.tile([P, SHIFT + entries], F32, name=f"silu{b}", align_bytes=BURST) for b in range(2)]
         products = [held.tile([P, entries], F32, name=f"product{b}", align_bytes=BURST) for b in range(2)]
 
         nc.sync.dma_start(gates[0][:], tab[0, 0:P, :])
@@ -45,7 +46,7 @@ def tile_lookup_glu_silu_out_kernel(tc, tab, offs, out):
         for b in range(2):
             for first, end in spans(SILUS[b]):
                 nc.scalar.activation(
-                    silus[b][:, first:end],
+                    silus[b][:, SHIFT + first : SHIFT + end],
                     gates[b][:].indirect(offsets[:, first // LANES : end // LANES]),
                     mybir.ActivationFunctionType.Silu,
                 )
@@ -53,7 +54,7 @@ def tile_lookup_glu_silu_out_kernel(tc, tab, offs, out):
                 nc.vector.tensor_tensor(
                     products[b][:, first:end],
                     values[b][:].indirect(offsets[:, first // LANES : end // LANES]),
-                    silus[b][:, first:end],
+                    silus[b][:, SHIFT + first : SHIFT + end],
                     mybir.AluOpType.mult,
                 )
             for first, end in spans(STORES[b]):

@@ -2,10 +2,10 @@ import concourse.mybir as mybir
 
 F32 = mybir.dt.float32
 U16 = mybir.dt.uint16
-U32 = mybir.dt.uint32
 
 P = 128
 BURST = 256
+PIECE = 2048
 SHIFT = 8
 LANES = 16
 SILUS = ((704, 704, 640), (704, 640, 704))
@@ -29,20 +29,20 @@ def tile_lookup_glu_silu_out_kernel(tc, tab, offs, out):
 
     with tc.tile_pool(name="held", bufs=1) as held:
         offsets = held.tile([P, entries // LANES], U16, name="offsets", align_bytes=BURST)
-        warm = held.tile([P, 1], U32, name="warm")
-        nc.scalar.activation(warm[:], warm[:], mybir.ActivationFunctionType.Silu, scale=0.0)
-
         gates = [held.tile([P, places], F32, name=f"gate{b}", align_bytes=BURST) for b in range(2)]
         values = [held.tile([P, places], F32, name=f"value{b}", align_bytes=BURST) for b in range(2)]
         silus = [held.tile([P, SHIFT + entries], F32, name=f"silu{b}", align_bytes=BURST) for b in range(2)]
         products = [held.tile([P, entries], F32, name=f"product{b}", align_bytes=BURST) for b in range(2)]
 
-        nc.sync.dma_start(gates[0][:], tab[0, 0:P, :])
-        nc.sync.dma_start(offsets[:], offs)
-        nc.sync.dma_start(values[0][:], tab[1, 0:P, :])
-        nc.sync.dma_start(gates[1][:], tab[0, P : 2 * P, :])
-        nc.sync.dma_start(values[1][:], tab[1, P : 2 * P, :])
+        warm = held.tile([P, 1], F32, name="warm")
+        nc.vector.memset(warm[:], 0.0)
+        nc.scalar.activation(warm[:], warm[:], mybir.ActivationFunctionType.Silu)
 
+        def load(tile, table, b):
+            nc.sync.dma_start(tile[:], tab[table, b * P : (b + 1) * P, :], max_dma_last_dim=PIECE)
+
+        load(gates[0], 0, 0)
+        nc.sync.dma_start(offsets[:], offs)
         for b in range(2):
             for first, end in spans(SILUS[b]):
                 nc.scalar.activation(
@@ -50,6 +50,10 @@ def tile_lookup_glu_silu_out_kernel(tc, tab, offs, out):
                     gates[b][:].indirect(offsets[:, first // LANES : end // LANES]),
                     mybir.ActivationFunctionType.Silu,
                 )
+            load(values[b], 1, b)
+            if b == 0:
+                load(gates[1], 0, 1)
+        for b in range(2):
             for first, end in spans(PRODUCTS[b]):
                 nc.vector.tensor_tensor(
                     products[b][:, first:end],

@@ -5,7 +5,6 @@ U16 = mybir.dt.uint16
 
 P = 128
 BURST = 256
-PIECE = 2048
 SHIFT = 8
 LANES = 16
 SILUS = ((704, 704, 640), (704, 640, 704))
@@ -39,7 +38,7 @@ def tile_lookup_glu_silu_out_kernel(tc, tab, offs, out):
         nc.scalar.activation(warm[:], warm[:], mybir.ActivationFunctionType.Silu)
 
         def load(tile, table, b):
-            nc.sync.dma_start(tile[:], tab[table, b * P : (b + 1) * P, :], max_dma_last_dim=PIECE)
+            nc.sync.dma_start(tile[:], tab[table, b * P : (b + 1) * P, :])
 
         load(gates[0], 0, 0)
         nc.sync.dma_start(offsets[:], offs)

@@ -7,9 +7,9 @@ P = 128
 BURST = 256
 SHIFT = 8
 LANES = 16
-SILUS = ((704, 704, 640), (704, 640, 704))
-PRODUCTS = ((704, 704, 640), (704, 640, 384, 192, 128))
-STORES = ((384, 320, 384, 320, 640), (384, 320, 640, 384, 192, 128))
+SILUS = ((640, 704, 704), (704, 640, 704))
+PRODUCTS = ((640, 704, 704), (704, 640, 384, 192, 128))
+STORES = ((640, 384, 320, 384, 320), (384, 320, 640, 384, 192, 128))
 
 
 def spans(widths):

@@ -9,7 +9,7 @@ SHIFT = 8
 LANES = 16
 SILUS = ((640, 704, 704), (704, 640, 704))
 PRODUCTS = ((640, 704, 704), (704, 640, 384, 192, 128))
-STORES = ((640, 384, 320, 384, 320), (384, 320, 640, 384, 192, 128))
+STORES = ((320, 320, 384, 320, 384, 320), (704, 640, 384, 192, 128))
 
 
 def spans(widths):

import concourse.mybir as mybir

F32 = mybir.dt.float32
U16 = mybir.dt.uint16

P = 128
BURST = 256
SHIFT = 8
LANES = 16
SILUS = ((640, 704, 704), (704, 640, 704))
PRODUCTS = ((640, 704, 704), (704, 640, 384, 192, 128))
STORES = ((320, 320, 384, 320, 384, 320), (704, 640, 384, 192, 128))


def spans(widths):
    first = 0
    cut = []
    for width in widths:
        cut.append((first, first + width))
        first += width
    return cut


def tile_lookup_glu_silu_out_kernel(tc, tab, offs, out):
    nc = tc.nc
    places = tab.shape[2]
    entries = out.shape[1]

    with tc.tile_pool(name="held", bufs=1) as held:
        offsets = held.tile([P, entries // LANES], U16, name="offsets", align_bytes=BURST)
        gates = [held.tile([P, places], F32, name=f"gate{b}", align_bytes=BURST) for b in range(2)]
        values = [held.tile([P, places], F32, name=f"value{b}", align_bytes=BURST) for b in range(2)]
        silus = [held.tile([P, SHIFT + entries], F32, name=f"silu{b}", align_bytes=BURST) for b in range(2)]
        products = [held.tile([P, entries], F32, name=f"product{b}", align_bytes=BURST) for b in range(2)]

        warm = held.tile([P, 1], F32, name="warm")
        nc.vector.memset(warm[:], 0.0)
        nc.scalar.activation(warm[:], warm[:], mybir.ActivationFunctionType.Silu)

        def load(tile, table, b):
            nc.sync.dma_start(tile[:], tab[table, b * P : (b + 1) * P, :])

        load(gates[0], 0, 0)
        nc.sync.dma_start(offsets[:], offs)
        for b in range(2):
            for first, end in spans(SILUS[b]):
                nc.scalar.activation(
                    silus[b][:, SHIFT + first : SHIFT + end],
                    gates[b][:].indirect(offsets[:, first // LANES : end // LANES]),
                    mybir.ActivationFunctionType.Silu,
                )
            load(values[b], 1, b)
            if b == 0:
                load(gates[1], 0, 1)
        for b in range(2):
            for first, end in spans(PRODUCTS[b]):
                nc.vector.tensor_tensor(
                    products[b][:, first:end],
                    values[b][:].indirect(offsets[:, first // LANES : end // LANES]),
                    silus[b][:, SHIFT + first : SHIFT + end],
                    mybir.AluOpType.mult,
                )
            for first, end in spans(STORES[b]):
                nc.sync.dma_start(out[b * P : (b + 1) * P, first:end], products[b][:, first:end])
